import numpy as np
import ml_dtypes


def mxq(x, axis, fmt="e4m3"):
    dtype, down = {"e4m3": (ml_dtypes.float8_e4m3fn, 7), "e5m2": (ml_dtypes.float8_e5m2, 14)}[fmt]
    v = np.moveaxis(np.asarray(x, np.float32).astype(ml_dtypes.bfloat16).astype(np.float64), axis, -1)
    blocks = v.reshape(v.shape[:-1] + (-1, 32))
    amax = np.abs(blocks).max(-1, keepdims=True)
    byte = np.maximum(np.where(amax > 0, np.frexp(amax)[1] - 1 + 127, 0) - down, 1)
    scale = np.exp2(byte - 127.0)
    codes = (blocks / scale).astype(np.float32).astype(dtype).astype(np.float64)
    return np.moveaxis((codes * scale).reshape(v.shape), -1, axis)


WIDE = False


def mx_kscale(k):
    if not WIDE:
        return np.ones(k)
    levels = np.array([10, -10, 5, -5, 0])
    if k % 512:
        return np.exp2(np.random.permutation(np.resize(levels, k // 32))).repeat(32)
    a = np.empty((k // 512, 16))
    for p in range(k // 512):
        a[p, :8] = np.random.permutation(np.resize(levels, 8))
        for g in range(8):
            far = levels[np.abs(levels - a[p, g]) >= 10]
            a[p, g + 8] = far[np.random.randint(len(far))]
    return np.exp2(a.ravel()).repeat(32)


def f64(x):
    return np.asarray(x).astype(np.float64)


E2M1 = np.array([0.0, 0.5, 1.0, 1.5, 2.0, 3.0, 4.0, 6.0, -0.0, -0.5, -1.0, -1.5, -2.0, -3.0, -4.0, -6.0])


def pack_weight(w, fmt):
    k, n = w.shape
    w = f64(np.asarray(w, np.float32).astype(ml_dtypes.bfloat16)).reshape(k // 32, 32, n)
    amax = np.abs(w).max(1)
    if fmt == "e4m3":
        byte = np.frexp(amax)[1] - 1 + 127 - 7
    else:
        mant, ex = np.frexp(amax / 6.0)
        byte = np.where(mant > 0.5, ex, ex - 1) + 127
    byte = np.clip(np.where(amax > 0, byte, 1), 1, 254)
    scaled = (w * np.exp2(127.0 - byte)[:, None, :]).reshape(k, n).astype(np.float32)
    by_word = np.ascontiguousarray(scaled.reshape(k // 512, 128, 4, n).transpose(0, 1, 3, 2))
    if fmt == "e4m3":
        words = by_word.astype(ml_dtypes.float8_e4m3fn).view(np.uint8)
    else:
        c = by_word.astype(ml_dtypes.float4_e2m1fn).view(np.uint8) & 0xF
        words = (c[..., 0::2] | (c[..., 1::2] << 4)).reshape(k // 512, 128, 2 * n)
    return np.ascontiguousarray(words), np.ascontiguousarray(byte.astype(np.uint8).reshape(k // 512, 16, n))


def unpack_weight(words, scales, fmt):
    g, _, n = scales.shape
    words = np.ascontiguousarray(words).reshape(g, 128, n, -1)
    if fmt == "e4m3":
        vals = words.view(ml_dtypes.float8_e4m3fn).astype(np.float64)
    else:
        nib = np.empty((g, 128, n, 4), np.uint8)
        nib[..., 0::2] = words & 0xF
        nib[..., 1::2] = words >> 4
        vals = E2M1[nib]
    vals = vals * np.repeat(np.exp2(scales.astype(np.float64) - 127.0), 8, axis=1)[..., None]
    return vals.transpose(0, 1, 3, 2).reshape(g * 512, n)


def planes(y):
    n, m = y.shape
    v = y.astype(np.float32).astype(ml_dtypes.bfloat16).astype(np.float64).reshape(n // 32, 32, m)
    top = np.abs(v).max(1)
    byte = np.clip(np.where(top > 0, np.frexp(top)[1] - 1 + 127 - 7, 1), 1, 254)
    codes = (v * np.exp2(127.0 - byte)[:, None, :]).reshape(n, m).astype(np.float32).astype(ml_dtypes.float8_e4m3fn).view(np.uint8)
    words = codes.reshape(n // 512, 128, 4, m).transpose(0, 1, 3, 2)
    return np.ascontiguousarray(words), np.ascontiguousarray(byte.astype(np.uint8).reshape(n // 512, 16, m))


def gelu(v):
    return 0.5 * v * (1.0 + np.tanh(np.sqrt(2.0 / np.pi) * (v + 0.044715 * v**3)))


O, K, R, M, T = 1024, 2048, 512, 1024, 512


def setup_inputs():
    n = np.random.standard_normal
    s = mx_kscale(K)[:, None]
    u = mx_kscale(R)[:, None]
    x = n((K, T)); x[:O] *= 6.0
    w = n((K, M)) / np.sqrt(K) / s; w[:O] /= 2.0
    p_w8 = pack_weight(w[:O], "e4m3")
    p_w4 = pack_weight(w[O:], "e2m1")
    p_up = pack_weight(n((R, M)) / np.sqrt(R) / u, "e2m1")
    return {
        "x": (x * s).astype(np.float32),
        "w8_words": p_w8[0],
        "w8_scales": p_w8[1],
        "w4_words": p_w4[0],
        "w4_scales": p_w4[1],
        "down": (0.3 * n((K, R)) / np.sqrt(K) / s * u.T).astype(np.float32),
        "up_words": p_up[0],
        "up_scales": p_up[1],
        "b": (0.3 * n(1024)).astype(np.float32),
    }


def reference(x, w8_words, w8_scales, w4_words, w4_scales, down, up_words, up_scales, b):
    x_ = mxq(f64(x), 0, "e4m3")
    w8_ = unpack_weight(w8_words, w8_scales, "e4m3")
    w4_ = unpack_weight(w4_words, w4_scales, "e2m1")
    down_ = mxq(f64(down), 0, "e4m3")
    up_ = unpack_weight(up_words, up_scales, "e2m1")
    h_ = mxq(down_.T @ x_, 0, "e4m3")
    y = w8_.T @ x_[:O] + w4_.T @ x_[O:] + up_.T @ h_
    out_0 = gelu(y + f64(b)[:, None])
    return (out_0,) + planes(out_0)

@@ -1,0 +1,286 @@
+from contextlib import ExitStack
+
+import concourse.mybir as mybir
+
+O, K, R, M, T = 1024, 2048, 512, 1024, 512
+FLOPS = 2 * T * (K * R + K * M + R * M)
+
+F32 = mybir.dt.float32
+BF16 = mybir.dt.bfloat16
+I32 = mybir.dt.int32
+U32 = mybir.dt.uint32
+U8 = mybir.dt.uint8
+FP8X4 = mybir.dt.float8_e4m3fn_x4
+FP4X4 = mybir.dt.float4_e2m1fn_x4
+GELU = mybir.ActivationFunctionType.Gelu_apprx_tanh
+
+P = 128
+PACK = 4
+KP = P * PACK
+PASSES = K // KP
+HALVES = M // KP
+QUADS = 4
+TQ = T // 4
+TH = T // 2
+
+X_VECTOR_COLS = 128
+LAST_A_VECTOR_COLS = 128
+LAST_B_VECTOR_COLS = 160
+
+
+def tile_mix_three_fm_pl_gelu_kernel(
+    tc, x, w8_words, w8_scales, w4_words, w4_scales, down, up_words, up_scales, b, out_0, out_1, out_2
+):
+    nc = tc.nc
+    with ExitStack() as ctx:
+        sb = ctx.enter_context(tc.tile_pool(name="sb", bufs=1))
+        ps = ctx.enter_context(tc.psum_pool(name="ps", bufs=1))
+        ctx.enter_context(tc.manual_schedule())
+
+        def tile(name, shape, dtype):
+            return sb.tile(shape, dtype, name=name, align_bytes=64)
+
+        last = PASSES - 1
+        x_raw = [tile("x_raw%d" % g, [P, PACK, T], F32) for g in range(last)]
+        xl_raw = [tile("xl_raw%d" % h, [P, PACK, TH], F32) for h in range(2)]
+        d_raw = [tile("d_raw%d" % g, [P, PACK, R], F32) for g in range(PASSES)]
+        x_bf = [tile("x_bf%d" % g, [P, T * PACK], BF16) for g in range(PASSES)]
+        d_bf = [tile("d_bf%d" % g, [P, R * PACK], BF16) for g in range(PASSES)]
+        x_q = [tile("x_q%d" % g, [P, T], U32) for g in range(PASSES)]
+        x_s = [tile("x_s%d" % g, [P, T], U8) for g in range(PASSES)]
+        d_q = [tile("d_q%d" % g, [P, R], U32) for g in range(PASSES)]
+        d_s = [tile("d_s%d" % g, [P, R], U8) for g in range(PASSES)]
+        w8_raw = [tile("w8_raw%d" % a, [P, 2, KP], U32) for a in range(HALVES)]
+        w8 = [tile("w8_%d" % a, [P, 2, KP], U32) for a in range(HALVES)]
+        w4_raw = [tile("w4_raw%d" % a, [P, 2, 2 * KP], U8) for a in range(HALVES)]
+        w4 = [tile("w4_%d" % a, [P, 2, 2 * KP], U8) for a in range(HALVES)]
+        up_raw = tile("up_raw", [P, 2 * M], U8)
+        up = [tile("up_%d" % a, [P, 2 * KP], U8) for a in range(HALVES)]
+        ws_raw = tile("ws_raw", [P, 3, M], U8)
+        ws = [tile("ws_%d" % a, [P, 3, KP], U8) for a in range(HALVES)]
+        bias = tile("bias", [P, HALVES, PACK], F32)
+        h_bf = tile("h_bf", [P, T * PACK], BF16)
+        h_q = tile("h_q", [P, T], U32)
+        h_s = tile("h_s", [P, T], U8)
+        y = [tile("y%d" % a, [P, PACK, T], F32) for a in range(HALVES)]
+        y_bf = [tile("y_bf%d" % a, [P, T * PACK], BF16) for a in range(HALVES)]
+        y_q = [tile("y_q%d" % a, [P, T], U32) for a in range(HALVES)]
+        y_s = tile("y_s", [P, HALVES, T], U8)
+
+        def rows(src, g):
+            return src[g * KP : (g + 1) * KP, :].rearrange("(p j) w -> p j w", j=PACK)
+
+        def load(dst, src):
+            nc.sync.dma_start(out=dst, in_=src)
+
+        ws_words = ws_raw[:].bitcast(I32)
+        scale_loads = []
+        for r in range(4):
+            src = w4_scales.bitcast(I32).rearrange("g (q r) n -> r q g n", r=4)[r]
+            scale_loads.append((ws_words[r:P:32, 0:2, :], src))
+        for q in range(QUADS):
+            src = w8_scales.bitcast(I32)[:, 4 * q : 4 * q + 4, :]
+            scale_loads.append((ws_words[32 * q + 4 : 32 * q + 12, 0, :], src))
+        for r in range(4):
+            src = up_scales.bitcast(I32)[0].rearrange("(q r) n -> r q n", r=4)[r]
+            scale_loads.append((ws_words[r:P:32, 2, :], src))
+
+        def load_w8(a):
+            src = w8_words[:, :, a * KP : (a + 1) * KP, :].rearrange("g p n i -> p g (n i)")
+            load(w8_raw[a][:].bitcast(I32), src.bitcast(I32))
+
+        def load_w4(a):
+            src = w4_words[:, :, 2 * a * KP : 2 * (a + 1) * KP].rearrange("g p c -> p g c")
+            load(w4_raw[a][:].bitcast(I32), src.bitcast(I32))
+
+        nc.vector.memset(ws_words, 0)
+        for g in range(2):
+            load(x_raw[g][:], rows(x, g))
+            load(d_raw[g][:], rows(down, g))
+            for dst, src in scale_loads[6 * g : 6 * g + 6]:
+                load(dst, src)
+        load_w8(0)
+        load_w4(0)
+        load(bias[:], b.rearrange("(a p i) -> p a i", p=P, i=PACK))
+        load(x_raw[2][:], rows(x, 2))
+        load(d_raw[2][:], rows(down, 2))
+        load(d_raw[3][:], rows(down, 3))
+        load(up_raw[:].bitcast(I32), up_words[0].bitcast(I32))
+        for h in range(2):
+            load(xl_raw[h][:], rows(x, last)[:, :, h * TH : (h + 1) * TH])
+        load_w8(1)
+        load_w4(1)
+
+        def interleave(copy, dst, src):
+            copy(
+                out=dst.rearrange("p (c i j) -> p c j i", i=4, j=PACK),
+                in_=src.rearrange("p j (c i) -> p c j i", i=4),
+            )
+
+        def round_cols(dst, src, vector_cols):
+            width = src.shape[2]
+            interleave(nc.vector.tensor_copy, dst[:, : PACK * vector_cols], src[:, :, :vector_cols])
+            interleave(nc.scalar.copy, dst[:, PACK * vector_cols : PACK * width], src[:, :, vector_cols:])
+
+        def round_down(g):
+            dst = d_bf[g][:].rearrange("p (i m j) -> p m j i", i=PACK, j=PACK)
+            src = d_raw[g][:].rearrange("p j (m i) -> p m j i", i=PACK)
+            nc.vector.tensor_copy(out=dst[:, :, :, 0:2], in_=src[:, :, :, 0:2])
+            nc.scalar.copy(out=dst[:, :, :, 2:4], in_=src[:, :, :, 2:4])
+
+        def quantize(codes, scales, src, c0, c1):
+            nc.vector.quantize_mx(
+                out=codes[:, c0:c1].bitcast(FP8X4), scales=scales[:, c0:c1], in_=src[:, PACK * c0 : PACK * c1]
+            )
+
+        def deal_scales(a):
+            src = ws_raw[:, :, a * KP : (a + 1) * KP].rearrange("p s (m i) -> p i s m", i=PACK)
+            nc.vector.tensor_copy(out=ws[a][:].rearrange("p s (i m) -> p i s m", i=PACK), in_=src)
+
+        def deal_w8(a):
+            nc.vector.tensor_copy(
+                out=w8[a][:].bitcast(I32).rearrange("p g (i m) -> p g m i", i=PACK),
+                in_=w8_raw[a][:].bitcast(I32).rearrange("p g (m i) -> p g m i", i=PACK),
+            )
+
+        def deal_w4(a):
+            nc.vector.tensor_copy(
+                out=w4[a][:].rearrange("p g (i m e) -> p g i m e", i=PACK, e=2),
+                in_=w4_raw[a][:].rearrange("p g (m i e) -> p g i m e", i=PACK, e=2),
+            )
+
+        def deal_up(a):
+            nc.vector.tensor_copy(
+                out=up[a][:].rearrange("p (i m e) -> p i m e", i=PACK, e=2),
+                in_=up_raw[:, 2 * a * KP : 2 * (a + 1) * KP].rearrange("p (m i e) -> p i m e", i=PACK, e=2),
+            )
+
+        h_acc = [ps.tile([P, PACK, TQ], F32, name="h_acc%d" % q, tag="bank%d" % q) for q in range(4)]
+
+        def h_pass(g, quarters):
+            for q in quarters:
+                for i in range(PACK):
+                    nc.tensor.matmul_mx(
+                        out=h_acc[q][:, i, :],
+                        lhsT=d_q[g][:, i * P : (i + 1) * P].bitcast(FP8X4),
+                        lhsT_scale=d_s[g][:, i * P : (i + 1) * P],
+                        rhs=x_q[g][:, q * TQ : (q + 1) * TQ].bitcast(FP8X4),
+                        rhs_scale=x_s[g][:, q * TQ : (q + 1) * TQ],
+                        start=(g == 0 and i == 0),
+                        stop=(g == last and i == PACK - 1),
+                    )
+
+        def y_pass(acc, a, i, g):
+            cols = slice(i * P, (i + 1) * P)
+            cols2 = slice(2 * i * P, 2 * (i + 1) * P)
+            if g < 2:
+                lhsT, lhsT_scale = w8[a][:, g, cols].bitcast(FP8X4), ws[a][4 + 4 * g : P, 0, cols]
+            elif g < PASSES:
+                lhsT, lhsT_scale = w4[a][:, g - 2, cols2].bitcast(FP4X4), ws[a][:, g - 2, cols]
+            else:
+                lhsT, lhsT_scale = up[a][:, cols2].bitcast(FP4X4), ws[a][:, 2, cols]
+            rhs, rhs_scale = (x_q[g], x_s[g]) if g < PASSES else (h_q, h_s)
+            nc.tensor.matmul_mx(
+                out=acc[:],
+                lhsT=lhsT,
+                lhsT_scale=lhsT_scale,
+                rhs=rhs[:].bitcast(FP8X4),
+                rhs_scale=rhs_scale[:],
+                start=(g == 0),
+                stop=(g == PASSES),
+            )
+
+        def h_out(q):
+            nc.scalar.copy(
+                out=h_bf[:, q * TQ * PACK : (q + 1) * TQ * PACK].rearrange("p (t i) -> p t i", i=PACK),
+                in_=h_acc[q][:].rearrange("p i t -> p t i"),
+            )
+
+        out_rows = out_0.rearrange("(a p i) t -> a p i t", p=P, i=PACK)
+
+        def gelu(acc, a, i, c0, c1):
+            nc.scalar.activation(out=y[a][:, i, c0:c1], in_=acc[:, c0:c1], func=GELU, bias=bias[:, a, i : i + 1])
+
+        def store_rows(a, i):
+            nc.sync.dma_start(out=out_rows[a, :, i, :], in_=y[a][:, i, :])
+
+        def store_words(a, c0, c1):
+            dst = out_1[a].rearrange("p t i -> p (t i)").bitcast(I32)
+            nc.sync.dma_start(out=dst[:, c0:c1], in_=y_q[a][:, c0:c1].bitcast(I32))
+
+        acc0 = [ps.tile([P, T], F32, name="acc0_%d" % i, tag="bank%d" % (4 + i)) for i in range(PACK)]
+
+        round_cols(x_bf[0], x_raw[0], X_VECTOR_COLS)
+        quantize(x_q[0], x_s[0], x_bf[0], 0, T)
+        round_down(0)
+        quantize(d_q[0], d_s[0], d_bf[0], 0, R)
+        h_pass(0, range(4))
+        round_cols(x_bf[1], x_raw[1], X_VECTOR_COLS)
+        quantize(x_q[1], x_s[1], x_bf[1], 0, T)
+        round_down(1)
+        deal_scales(0)
+        quantize(d_q[1], d_s[1], d_bf[1], 0, R)
+        h_pass(1, range(4))
+        deal_w8(0)
+        deal_w4(0)
+        for g in range(2):
+            for i in range(PACK):
+                y_pass(acc0[i], 0, i, g)
+        round_cols(x_bf[2], x_raw[2], X_VECTOR_COLS)
+        deal_scales(1)
+        quantize(x_q[2], x_s[2], x_bf[2], 0, T)
+        round_down(2)
+        quantize(d_q[2], d_s[2], d_bf[2], 0, R)
+        h_pass(2, range(4))
+        for i in range(PACK):
+            y_pass(acc0[i], 0, i, 2)
+        round_down(3)
+        quantize(d_q[3], d_s[3], d_bf[3], 0, R)
+        for h, vector_cols in enumerate((LAST_A_VECTOR_COLS, LAST_B_VECTOR_COLS)):
+            round_cols(x_bf[last][:, h * TH * PACK : (h + 1) * TH * PACK], xl_raw[h], vector_cols)
+            quantize(x_q[last], x_s[last], x_bf[last], h * TH, (h + 1) * TH)
+            h_pass(last, (2 * h, 2 * h + 1))
+        for q in range(4):
+            h_out(q)
+        for i in range(PACK):
+            y_pass(acc0[i], 0, i, last)
+        deal_up(0)
+        deal_w8(1)
+        deal_w4(1)
+        quantize(h_q, h_s, h_bf, 0, T)
+        deal_up(1)
+
+        acc1 = [ps.tile([P, T], F32, name="acc1_%d" % i, tag="bank%d" % i) for i in range(PACK)]
+        for g in range(PASSES):
+            y_pass(acc1[0], 1, 0, g)
+        for i in range(PACK):
+            y_pass(acc0[i], 0, i, PASSES)
+            gelu(acc0[i], 0, i, 0, T)
+            store_rows(0, i)
+        y_pass(acc1[0], 1, 0, PASSES)
+        interleave(nc.vector.tensor_copy, y_bf[0][:], y[0][:])
+        quantize(y_q[0], y_s[:, 0, :], y_bf[0], 0, T)
+        for i in range(PACK):
+            if i > 0:
+                for g in range(PASSES + 1):
+                    y_pass(acc1[i], 1, i, g)
+            if i < PACK - 1:
+                gelu(acc1[i], 1, i, 0, T)
+            else:
+                gelu(acc1[i], 1, i, 0, TH)
+                gelu(acc1[i], 1, i, TH, T)
+            if i == 1:
+                store_words(0, 0, T)
+            store_rows(1, i)
+        interleave(nc.vector.tensor_copy, y_bf[1][:, : TH * PACK], y[1][:, :, :TH])
+        interleave(nc.vector.tensor_copy, y_bf[1][:, TH * PACK : 3 * TQ * PACK], y[1][:, :, TH : 3 * TQ])
+        interleave(nc.scalar.copy, y_bf[1][:, 3 * TQ * PACK :], y[1][:, :, 3 * TQ :])
+        for h in range(2):
+            quantize(y_q[1], y_s[:, 1, :], y_bf[1], h * TH, (h + 1) * TH)
+            store_words(1, h * TH, (h + 1) * TH)
+        for q in range(QUADS):
+            eng = nc.sync if q % 2 == 0 else nc.scalar
+            eng.dma_start(
+                out=out_2.bitcast(I32)[:, 4 * q : 4 * q + 4, :].rearrange("a r t -> r a t"),
+                in_=y_s[32 * q : 32 * q + 4, :, :].bitcast(I32),
+            )

@@ -24,8 +24,8 @@ TQ = T // 4
 TH = T // 2
 
 X_VECTOR_COLS = 128
-LAST_A_VECTOR_COLS = 128
-LAST_B_VECTOR_COLS = 160
+LAST_VECTOR_COLS = 256
+OUT_VECTOR_COLS = 128
 
 
 def tile_mix_three_fm_pl_gelu_kernel(
@@ -41,11 +41,11 @@ def tile_mix_three_fm_pl_gelu_kernel(
             return sb.tile(shape, dtype, name=name, align_bytes=64)
 
         last = PASSES - 1
-        x_raw = [tile("x_raw%d" % g, [P, PACK, T], F32) for g in range(last)]
-        xl_raw = [tile("xl_raw%d" % h, [P, PACK, TH], F32) for h in range(2)]
-        d_raw = [tile("d_raw%d" % g, [P, PACK, R], F32) for g in range(PASSES)]
+        x_raw = [tile("x_raw%d" % g, [P, PACK, T], F32) for g in range(PASSES)]
+        d_raw = [tile("d_raw%d" % g, [P, PACK, R], F32) for g in range(last)]
+        dl_raw = [tile("dl_raw%d" % h, [P, PACK, R // 2], F32) for h in range(2)]
         x_bf = [tile("x_bf%d" % g, [P, T * PACK], BF16) for g in range(PASSES)]
-        d_bf = [tile("d_bf%d" % g, [P, R * PACK], BF16) for g in range(PASSES)]
+        d_bf = [[tile("d_bf%d_%d" % (g, u), [P, 2 * R], BF16) for u in range(2)] for g in range(PASSES)]
         x_q = [tile("x_q%d" % g, [P, T], U32) for g in range(PASSES)]
         x_s = [tile("x_s%d" % g, [P, T], U8) for g in range(PASSES)]
         d_q = [tile("d_q%d" % g, [P, R], U32) for g in range(PASSES)]
@@ -54,10 +54,12 @@ def tile_mix_three_fm_pl_gelu_kernel(
         w8 = [tile("w8_%d" % a, [P, 2, KP], U32) for a in range(HALVES)]
         w4_raw = [tile("w4_raw%d" % a, [P, 2, 2 * KP], U8) for a in range(HALVES)]
         w4 = [tile("w4_%d" % a, [P, 2, 2 * KP], U8) for a in range(HALVES)]
-        up_raw = tile("up_raw", [P, 2 * M], U8)
+        up_raw = [tile("up_raw%d" % a, [P, 2 * KP], U8) for a in range(HALVES)]
         up = [tile("up_%d" % a, [P, 2 * KP], U8) for a in range(HALVES)]
-        ws_raw = tile("ws_raw", [P, 3, M], U8)
-        ws = [tile("ws_%d" % a, [P, 3, KP], U8) for a in range(HALVES)]
+        ws_raw = tile("ws_raw", [P, 2, M], U8)
+        ws = [tile("ws_%d" % a, [P, 2, KP], U8) for a in range(HALVES)]
+        us_raw = tile("us_raw", [P, M], U8)
+        us = tile("us", [P, M], U8)
         bias = tile("bias", [P, HALVES, PACK], F32)
         h_bf = tile("h_bf", [P, T * PACK], BF16)
         h_q = tile("h_q", [P, T], U32)
@@ -74,16 +76,17 @@ def tile_mix_three_fm_pl_gelu_kernel(
             nc.sync.dma_start(out=dst, in_=src)
 
         ws_words = ws_raw[:].bitcast(I32)
+        us_words = us_raw[:].bitcast(I32)
         scale_loads = []
         for r in range(4):
+            src = w8_scales.bitcast(I32).rearrange("g (q r) n -> r q g n", r=4)[r]
+            scale_loads.append((ws_words[4 + r : P : 32, :, :], src))
+        for r in range(4):
             src = w4_scales.bitcast(I32).rearrange("g (q r) n -> r q g n", r=4)[r]
-            scale_loads.append((ws_words[r:P:32, 0:2, :], src))
-        for q in range(QUADS):
-            src = w8_scales.bitcast(I32)[:, 4 * q : 4 * q + 4, :]
-            scale_loads.append((ws_words[32 * q + 4 : 32 * q + 12, 0, :], src))
+            scale_loads.append((ws_words[r:P:32, :, :], src))
         for r in range(4):
             src = up_scales.bitcast(I32)[0].rearrange("(q r) n -> r q n", r=4)[r]
-            scale_loads.append((ws_words[r:P:32, 2, :], src))
+            scale_loads.append((us_words[r:P:32, :], src))
 
         def load_w8(a):
             src = w8_words[:, :, a * KP : (a + 1) * KP, :].rearrange("g p n i -> p g (n i)")
@@ -93,23 +96,32 @@ def tile_mix_three_fm_pl_gelu_kernel(
             src = w4_words[:, :, 2 * a * KP : 2 * (a + 1) * KP].rearrange("g p c -> p g c")
             load(w4_raw[a][:].bitcast(I32), src.bitcast(I32))
 
+        def load_up(a):
+            load(up_raw[a][:].bitcast(I32), up_words[0, :, 2 * a * KP : 2 * (a + 1) * KP].bitcast(I32))
+
+        warm = tile("warm", [P, 8], F32)
         nc.vector.memset(ws_words, 0)
-        for g in range(2):
-            load(x_raw[g][:], rows(x, g))
-            load(d_raw[g][:], rows(down, g))
-            for dst, src in scale_loads[6 * g : 6 * g + 6]:
-                load(dst, src)
+        nc.vector.memset(us_words, 0)
+        nc.vector.memset(warm[:], 0.0)
+        nc.scalar.activation(out=warm[:], in_=warm[:], func=GELU)
+        for dst, src in scale_loads:
+            nc.gpsimd.dma_start(out=dst, in_=src)
+        load(x_raw[0][:], rows(x, 0))
+        load(d_raw[0][:], rows(down, 0))
         load_w8(0)
         load_w4(0)
+        load_up(0)
         load(bias[:], b.rearrange("(a p i) -> p a i", p=P, i=PACK))
+        load(x_raw[1][:], rows(x, 1))
+        load(d_raw[1][:], rows(down, 1))
         load(x_raw[2][:], rows(x, 2))
         load(d_raw[2][:], rows(down, 2))
-        load(d_raw[3][:], rows(down, 3))
-        load(up_raw[:].bitcast(I32), up_words[0].bitcast(I32))
+        load(x_raw[last][:], rows(x, last))
         for h in range(2):
-            load(xl_raw[h][:], rows(x, last)[:, :, h * TH : (h + 1) * TH])
+            load(dl_raw[h][:], rows(down, last)[:, :, h * R // 2 : (h + 1) * R // 2])
         load_w8(1)
         load_w4(1)
+        load_up(1)
 
         def interleave(copy, dst, src):
             copy(
@@ -122,11 +134,16 @@ def tile_mix_three_fm_pl_gelu_kernel(
             interleave(nc.vector.tensor_copy, dst[:, : PACK * vector_cols], src[:, :, :vector_cols])
             interleave(nc.scalar.copy, dst[:, PACK * vector_cols : PACK * width], src[:, :, vector_cols:])
 
-        def round_down(g):
-            dst = d_bf[g][:].rearrange("p (i m j) -> p m j i", i=PACK, j=PACK)
-            src = d_raw[g][:].rearrange("p j (m i) -> p m j i", i=PACK)
-            nc.vector.tensor_copy(out=dst[:, :, :, 0:2], in_=src[:, :, :, 0:2])
-            nc.scalar.copy(out=dst[:, :, :, 2:4], in_=src[:, :, :, 2:4])
+        def round_down(g, raw, m0, m1):
+            src = raw[:].rearrange("p j (m i) -> p m j i", i=PACK)
+            for u, copy in enumerate((nc.vector.tensor_copy, nc.scalar.copy)):
+                dst = d_bf[g][u][:].rearrange("p (i m j) -> p m j i", i=2, j=PACK)
+                copy(out=dst[:, m0:m1, :, :], in_=src[:, :, :, 2 * u : 2 * u + 2])
+
+        def quantize_down(g):
+            for u in range(2):
+                cols = slice(u * R // 2, (u + 1) * R // 2)
+                nc.vector.quantize_mx(out=d_q[g][:, cols].bitcast(FP8X4), scales=d_s[g][:, cols], in_=d_bf[g][u][:])
 
         def quantize(codes, scales, src, c0, c1):
             nc.vector.quantize_mx(
@@ -136,6 +153,12 @@ def tile_mix_three_fm_pl_gelu_kernel(
         def deal_scales(a):
             src = ws_raw[:, :, a * KP : (a + 1) * KP].rearrange("p s (m i) -> p i s m", i=PACK)
             nc.vector.tensor_copy(out=ws[a][:].rearrange("p s (i m) -> p i s m", i=PACK), in_=src)
+
+        def deal_up_scales():
+            nc.vector.tensor_copy(
+                out=us[:].rearrange("p (a i m) -> p i a m", a=HALVES, i=PACK),
+                in_=us_raw[:].rearrange("p (a m i) -> p i a m", a=HALVES, i=PACK),
+            )
 
         def deal_w8(a):
             nc.vector.tensor_copy(
@@ -152,14 +175,14 @@ def tile_mix_three_fm_pl_gelu_kernel(
         def deal_up(a):
             nc.vector.tensor_copy(
                 out=up[a][:].rearrange("p (i m e) -> p i m e", i=PACK, e=2),
-                in_=up_raw[:, 2 * a * KP : 2 * (a + 1) * KP].rearrange("p (m i e) -> p i m e", i=PACK, e=2),
+                in_=up_raw[a][:].rearrange("p (m i e) -> p i m e", i=PACK, e=2),
             )
 
         h_acc = [ps.tile([P, PACK, TQ], F32, name="h_acc%d" % q, tag="bank%d" % q) for q in range(4)]
 
-        def h_pass(g, quarters):
-            for q in quarters:
-                for i in range(PACK):
+        def h_pass(g, tiles):
+            for q in range(4):
+                for i in tiles:
                     nc.tensor.matmul_mx(
                         out=h_acc[q][:, i, :],
                         lhsT=d_q[g][:, i * P : (i + 1) * P].bitcast(FP8X4),
@@ -170,28 +193,31 @@ def tile_mix_three_fm_pl_gelu_kernel(
                         stop=(g == last and i == PACK - 1),
                     )
 
-        def y_pass(acc, a, i, g):
+        def y_pass(acc, a, i, g, c0=0, c1=T):
             cols = slice(i * P, (i + 1) * P)
             cols2 = slice(2 * i * P, 2 * (i + 1) * P)
             if g < 2:
-                lhsT, lhsT_scale = w8[a][:, g, cols].bitcast(FP8X4), ws[a][4 + 4 * g : P, 0, cols]
+                lhsT, lhsT_scale = w8[a][:, g, cols].bitcast(FP8X4), ws[a][4:P, g, cols]
             elif g < PASSES:
                 lhsT, lhsT_scale = w4[a][:, g - 2, cols2].bitcast(FP4X4), ws[a][:, g - 2, cols]
             else:
-                lhsT, lhsT_scale = up[a][:, cols2].bitcast(FP4X4), ws[a][:, 2, cols]
+                lhsT, lhsT_scale = up[a][:, cols2].bitcast(FP4X4), us[:, a * KP + i * P : a * KP + (i + 1) * P]
             rhs, rhs_scale = (x_q[g], x_s[g]) if g < PASSES else (h_q, h_s)
-            nc.tensor.matmul_mx(
-                out=acc[:],
-                lhsT=lhsT,
-                lhsT_scale=lhsT_scale,
-                rhs=rhs[:].bitcast(FP8X4),
-                rhs_scale=rhs_scale[:],
-                start=(g == 0),
-                stop=(g == PASSES),
-            )
+            step = TQ if g >= 2 and c1 - c0 < T else c1 - c0
+            for c in range(c0, c1, step):
+                nc.tensor.matmul_mx(
+                    out=acc[:, c - c0 : c - c0 + step],
+                    lhsT=lhsT,
+                    lhsT_scale=lhsT_scale,
+                    rhs=rhs[:, c : c + step].bitcast(FP8X4),
+                    rhs_scale=rhs_scale[:, c : c + step],
+                    start=(g == 0),
+                    stop=(g == PASSES and c + step == c1),
+                )
 
         def h_out(q):
-            nc.scalar.copy(
+            copy = nc.scalar.copy if q % 2 == 0 else nc.vector.tensor_copy
+            copy(
                 out=h_bf[:, q * TQ * PACK : (q + 1) * TQ * PACK].rearrange("p (t i) -> p t i", i=PACK),
                 in_=h_acc[q][:].rearrange("p i t -> p t i"),
             )
@@ -199,10 +225,10 @@ def tile_mix_three_fm_pl_gelu_kernel(
         out_rows = out_0.rearrange("(a p i) t -> a p i t", p=P, i=PACK)
 
         def gelu(acc, a, i, c0, c1):
-            nc.scalar.activation(out=y[a][:, i, c0:c1], in_=acc[:, c0:c1], func=GELU, bias=bias[:, a, i : i + 1])
+            nc.scalar.activation(out=y[a][:, i, c0:c1], in_=acc[:], func=GELU, bias=bias[:, a, i : i + 1])
 
-        def store_rows(a, i):
-            nc.sync.dma_start(out=out_rows[a, :, i, :], in_=y[a][:, i, :])
+        def store_rows(a, i, c0=0, c1=T):
+            nc.sync.dma_start(out=out_rows[a, :, i, c0:c1], in_=y[a][:, i, c0:c1])
 
         def store_words(a, c0, c1):
             dst = out_1[a].rearrange("p t i -> p (t i)").bitcast(I32)
@@ -212,69 +238,78 @@ def tile_mix_three_fm_pl_gelu_kernel(
 
         round_cols(x_bf[0], x_raw[0], X_VECTOR_COLS)
         quantize(x_q[0], x_s[0], x_bf[0], 0, T)
-        round_down(0)
-        quantize(d_q[0], d_s[0], d_bf[0], 0, R)
-        h_pass(0, range(4))
-        round_cols(x_bf[1], x_raw[1], X_VECTOR_COLS)
-        quantize(x_q[1], x_s[1], x_bf[1], 0, T)
-        round_down(1)
-        deal_scales(0)
-        quantize(d_q[1], d_s[1], d_bf[1], 0, R)
-        h_pass(1, range(4))
+        round_down(0, d_raw[0], 0, P)
+        quantize_down(0)
+        h_pass(0, range(PACK))
         deal_w8(0)
         deal_w4(0)
+        deal_up(0)
+        round_cols(x_bf[1], x_raw[1], X_VECTOR_COLS)
+        deal_scales(0)
+        quantize(x_q[1], x_s[1], x_bf[1], 0, T)
         for g in range(2):
             for i in range(PACK):
                 y_pass(acc0[i], 0, i, g)
+        round_down(1, d_raw[1], 0, P)
+        deal_up_scales()
+        quantize_down(1)
+        h_pass(1, range(PACK))
         round_cols(x_bf[2], x_raw[2], X_VECTOR_COLS)
         deal_scales(1)
         quantize(x_q[2], x_s[2], x_bf[2], 0, T)
-        round_down(2)
-        quantize(d_q[2], d_s[2], d_bf[2], 0, R)
-        h_pass(2, range(4))
         for i in range(PACK):
             y_pass(acc0[i], 0, i, 2)
-        round_down(3)
-        quantize(d_q[3], d_s[3], d_bf[3], 0, R)
-        for h, vector_cols in enumerate((LAST_A_VECTOR_COLS, LAST_B_VECTOR_COLS)):
-            round_cols(x_bf[last][:, h * TH * PACK : (h + 1) * TH * PACK], xl_raw[h], vector_cols)
-            quantize(x_q[last], x_s[last], x_bf[last], h * TH, (h + 1) * TH)
-            h_pass(last, (2 * h, 2 * h + 1))
-        for q in range(4):
-            h_out(q)
+        round_down(2, d_raw[2], 0, P)
+        quantize_down(2)
+        h_pass(2, range(PACK))
+        round_cols(x_bf[last], x_raw[last], LAST_VECTOR_COLS)
+        quantize(x_q[last], x_s[last], x_bf[last], 0, T)
         for i in range(PACK):
             y_pass(acc0[i], 0, i, last)
-        deal_up(0)
+        for h in range(2):
+            round_down(last, dl_raw[h], h * P // 2, (h + 1) * P // 2)
+        quantize_down(last)
+        for u in range(2):
+            h_pass(last, (2 * u, 2 * u + 1))
         deal_w8(1)
-        deal_w4(1)
+        for q in range(4):
+            h_out(q)
         quantize(h_q, h_s, h_bf, 0, T)
+        deal_w4(1)
         deal_up(1)
 
-        acc1 = [ps.tile([P, T], F32, name="acc1_%d" % i, tag="bank%d" % i) for i in range(PACK)]
-        for g in range(PASSES):
-            y_pass(acc1[0], 1, 0, g)
+        top = PACK - 1
+        acc1 = [ps.tile([P, T], F32, name="acc1_%d" % i, tag="bank%d" % i) for i in range(top)]
+        acc_left = ps.tile([P, TH], F32, name="acc_left", tag="bank%d" % top)
+        for i in range(top):
+            for g in range(2):
+                y_pass(acc1[i], 1, i, g)
         for i in range(PACK):
             y_pass(acc0[i], 0, i, PASSES)
             gelu(acc0[i], 0, i, 0, T)
             store_rows(0, i)
-        y_pass(acc1[0], 1, 0, PASSES)
+        for g in range(2):
+            y_pass(acc_left, 1, top, g, 0, TH)
         interleave(nc.vector.tensor_copy, y_bf[0][:], y[0][:])
         quantize(y_q[0], y_s[:, 0, :], y_bf[0], 0, T)
-        for i in range(PACK):
-            if i > 0:
-                for g in range(PASSES + 1):
-                    y_pass(acc1[i], 1, i, g)
-            if i < PACK - 1:
-                gelu(acc1[i], 1, i, 0, T)
-            else:
-                gelu(acc1[i], 1, i, 0, TH)
-                gelu(acc1[i], 1, i, TH, T)
+        for i in range(top):
+            for g in range(2, PASSES + 1):
+                y_pass(acc1[i], 1, i, g)
+            gelu(acc1[i], 1, i, 0, T)
+            store_rows(1, i)
             if i == 1:
                 store_words(0, 0, T)
-            store_rows(1, i)
+        for g in range(2, PASSES + 1):
+            y_pass(acc_left, 1, top, g, 0, TH)
+        gelu(acc_left, 1, top, 0, TH)
+        store_rows(1, top, 0, TH)
+        acc_right = ps.tile([P, TH], F32, name="acc_right", tag="bank4")
+        for g in range(PASSES + 1):
+            y_pass(acc_right, 1, top, g, TH, T)
         interleave(nc.vector.tensor_copy, y_bf[1][:, : TH * PACK], y[1][:, :, :TH])
-        interleave(nc.vector.tensor_copy, y_bf[1][:, TH * PACK : 3 * TQ * PACK], y[1][:, :, TH : 3 * TQ])
-        interleave(nc.scalar.copy, y_bf[1][:, 3 * TQ * PACK :], y[1][:, :, 3 * TQ :])
+        gelu(acc_right, 1, top, TH, T)
+        store_rows(1, top, TH, T)
+        round_cols(y_bf[1][:, TH * PACK :], y[1][:, :, TH:], OUT_VECTOR_COLS)
         for h in range(2):
             quantize(y_q[1], y_s[:, 1, :], y_bf[1], h * TH, (h + 1) * TH)
             store_words(1, h * TH, (h + 1) * TH)

@@ -2,7 +2,7 @@ from contextlib import ExitStack
 
 import concourse.mybir as mybir
 
-O, K, R, M, T = 1024, 2048, 512, 1024, 512
+K, R, M, T = 2048, 512, 1024, 512
 FLOPS = 2 * T * (K * R + K * M + R * M)
 
 F32 = mybir.dt.float32
@@ -18,14 +18,19 @@ P = 128
 PACK = 4
 KP = P * PACK
 PASSES = K // KP
+W8_PASSES = 2
+UP_PASS = PASSES
+LAST = PASSES - 1
+TOP = PACK - 1
 HALVES = M // KP
-QUADS = 4
+QUAD = 32
+W8_ROW = 4
 TQ = T // 4
 TH = T // 2
+MH = P // 2
 
-X_VECTOR_COLS = 128
-LAST_VECTOR_COLS = 256
-OUT_VECTOR_COLS = 128
+X_VECTOR_COLS = (0, 0, 128, 320)
+OUT_VECTOR_COLS = 160
 
 
 def tile_mix_three_fm_pl_gelu_kernel(
@@ -40,99 +45,98 @@ def tile_mix_three_fm_pl_gelu_kernel(
         def tile(name, shape, dtype):
             return sb.tile(shape, dtype, name=name, align_bytes=64)
 
-        last = PASSES - 1
-        x_raw = [tile("x_raw%d" % g, [P, PACK, T], F32) for g in range(PASSES)]
-        d_raw = [tile("d_raw%d" % g, [P, PACK, R], F32) for g in range(last)]
-        dl_raw = [tile("dl_raw%d" % h, [P, PACK, R // 2], F32) for h in range(2)]
-        x_bf = [tile("x_bf%d" % g, [P, T * PACK], BF16) for g in range(PASSES)]
-        d_bf = [[tile("d_bf%d_%d" % (g, u), [P, 2 * R], BF16) for u in range(2)] for g in range(PASSES)]
-        x_q = [tile("x_q%d" % g, [P, T], U32) for g in range(PASSES)]
-        x_s = [tile("x_s%d" % g, [P, T], U8) for g in range(PASSES)]
-        d_q = [tile("d_q%d" % g, [P, R], U32) for g in range(PASSES)]
-        d_s = [tile("d_s%d" % g, [P, R], U8) for g in range(PASSES)]
-        w8_raw = [tile("w8_raw%d" % a, [P, 2, KP], U32) for a in range(HALVES)]
-        w8 = [tile("w8_%d" % a, [P, 2, KP], U32) for a in range(HALVES)]
-        w4_raw = [tile("w4_raw%d" % a, [P, 2, 2 * KP], U8) for a in range(HALVES)]
-        w4 = [tile("w4_%d" % a, [P, 2, 2 * KP], U8) for a in range(HALVES)]
-        up_raw = [tile("up_raw%d" % a, [P, 2 * KP], U8) for a in range(HALVES)]
-        up = [tile("up_%d" % a, [P, 2 * KP], U8) for a in range(HALVES)]
+        def tiles(name, count, shape, dtype):
+            return [tile("%s%d" % (name, n), shape, dtype) for n in range(count)]
+
+        x_raw = tiles("x_raw", PASSES, [P, PACK, T], F32)
+        x_bf = tiles("x_bf", PASSES, [P, T * PACK], BF16)
+        x_q = tiles("x_q", PASSES, [P, T], U32)
+        x_s = tiles("x_s", PASSES, [P, T], U8)
+        d_raw = tiles("d_raw", LAST, [P, PACK, R], F32)
+        d_last_raw = tiles("d_last_raw", 2, [P, PACK, R // 2], F32)
+        d_bf = [tiles("d_bf%d_" % g, 2, [P, 2 * KP], BF16) for g in range(PASSES)]
+        d_q = tiles("d_q", PASSES, [P, R], U32)
+        d_s = tiles("d_s", PASSES, [P, R], U8)
+        w8_raw = tiles("w8_raw", HALVES, [P, 2, KP], U32)
+        w8 = tiles("w8_", HALVES, [P, 2, KP], U32)
+        w4_raw = tiles("w4_raw", HALVES, [P, 2, 2 * KP], U8)
+        w4 = [tiles("w4_%d_" % a, 2, [P, 2, KP], U8) for a in range(HALVES)]
+        up_raw = tiles("up_raw", HALVES, [P, 2 * KP], U8)
+        up = [tiles("up_%d_" % a, 2, [P, KP], U8) for a in range(HALVES)]
         ws_raw = tile("ws_raw", [P, 2, M], U8)
-        ws = [tile("ws_%d" % a, [P, 2, KP], U8) for a in range(HALVES)]
+        ws = tiles("ws_", HALVES, [P, 2, KP], U8)
         us_raw = tile("us_raw", [P, M], U8)
         us = tile("us", [P, M], U8)
         bias = tile("bias", [P, HALVES, PACK], F32)
+        warm = tile("warm", [P, 8], F32)
         h_bf = tile("h_bf", [P, T * PACK], BF16)
         h_q = tile("h_q", [P, T], U32)
         h_s = tile("h_s", [P, T], U8)
-        y = [tile("y%d" % a, [P, PACK, T], F32) for a in range(HALVES)]
-        y_bf = [tile("y_bf%d" % a, [P, T * PACK], BF16) for a in range(HALVES)]
-        y_q = [tile("y_q%d" % a, [P, T], U32) for a in range(HALVES)]
+        y = tiles("y", HALVES, [P, PACK, T], F32)
+        y_bf = tiles("y_bf", HALVES, [P, T * PACK], BF16)
+        y_q = tiles("y_q", HALVES, [P, T], U32)
         y_s = tile("y_s", [P, HALVES, T], U8)
 
-        def rows(src, g):
-            return src[g * KP : (g + 1) * KP, :].rearrange("(p j) w -> p j w", j=PACK)
+        def pass_rows(src, g):
+            return src[g * KP : (g + 1) * KP, :].rearrange("(p j) c -> p j c", j=PACK)
 
         def load(dst, src):
             nc.sync.dma_start(out=dst, in_=src)
 
-        ws_words = ws_raw[:].bitcast(I32)
-        us_words = us_raw[:].bitcast(I32)
-        scale_loads = []
-        for r in range(4):
-            src = w8_scales.bitcast(I32).rearrange("g (q r) n -> r q g n", r=4)[r]
-            scale_loads.append((ws_words[4 + r : P : 32, :, :], src))
-        for r in range(4):
-            src = w4_scales.bitcast(I32).rearrange("g (q r) n -> r q g n", r=4)[r]
-            scale_loads.append((ws_words[r:P:32, :, :], src))
-        for r in range(4):
-            src = up_scales.bitcast(I32)[0].rearrange("(q r) n -> r q n", r=4)[r]
-            scale_loads.append((us_words[r:P:32, :], src))
-
-        def load_w8(a):
-            src = w8_words[:, :, a * KP : (a + 1) * KP, :].rearrange("g p n i -> p g (n i)")
+        def load_weights(a):
+            src = w8_words[:, :, a * KP : (a + 1) * KP, :].rearrange("g p n j -> p g (n j)")
             load(w8_raw[a][:].bitcast(I32), src.bitcast(I32))
-
-        def load_w4(a):
             src = w4_words[:, :, 2 * a * KP : 2 * (a + 1) * KP].rearrange("g p c -> p g c")
             load(w4_raw[a][:].bitcast(I32), src.bitcast(I32))
-
-        def load_up(a):
             load(up_raw[a][:].bitcast(I32), up_words[0, :, 2 * a * KP : 2 * (a + 1) * KP].bitcast(I32))
 
-        warm = tile("warm", [P, 8], F32)
+        def load_scales(engine, dst, first_row, scales):
+            src = scales.bitcast(I32).rearrange("g (q r) n -> r q g n", r=4)
+            for r in range(4):
+                engine.dma_start(out=dst[first_row + r : P : QUAD], in_=src[r])
+
+        ws_words = ws_raw[:].bitcast(I32)
+        us_words = us_raw[:].bitcast(I32).rearrange("p (g n) -> p g n", g=1)
         nc.vector.memset(ws_words, 0)
         nc.vector.memset(us_words, 0)
         nc.vector.memset(warm[:], 0.0)
         nc.scalar.activation(out=warm[:], in_=warm[:], func=GELU)
-        for dst, src in scale_loads:
-            nc.gpsimd.dma_start(out=dst, in_=src)
-        load(x_raw[0][:], rows(x, 0))
-        load(d_raw[0][:], rows(down, 0))
-        load_w8(0)
-        load_w4(0)
-        load_up(0)
+
+        load_scales(nc.gpsimd, ws_words, W8_ROW, w8_scales)
+        load_weights(0)
+        load(x_raw[0][:], pass_rows(x, 0))
+        load_scales(nc.scalar, ws_words, 0, w4_scales)
+        load(d_raw[0][:], pass_rows(down, 0))
+        load(x_raw[1][:], pass_rows(x, 1))
+        load(d_raw[1][:], pass_rows(down, 1))
+        load_scales(nc.sync, us_words, 0, up_scales)
+        load(x_raw[2][:], pass_rows(x, 2))
+        load(d_raw[2][:], pass_rows(down, 2))
+        load(x_raw[LAST][:], pass_rows(x, LAST))
+        for half in range(2):
+            load(d_last_raw[half][:], pass_rows(down, LAST)[:, :, half * R // 2 : (half + 1) * R // 2])
+        load_weights(1)
         load(bias[:], b.rearrange("(a p i) -> p a i", p=P, i=PACK))
-        load(x_raw[1][:], rows(x, 1))
-        load(d_raw[1][:], rows(down, 1))
-        load(x_raw[2][:], rows(x, 2))
-        load(d_raw[2][:], rows(down, 2))
-        load(x_raw[last][:], rows(x, last))
-        for h in range(2):
-            load(dl_raw[h][:], rows(down, last)[:, :, h * R // 2 : (h + 1) * R // 2])
-        load_w8(1)
-        load_w4(1)
-        load_up(1)
 
         def interleave(copy, dst, src):
             copy(
-                out=dst.rearrange("p (c i j) -> p c j i", i=4, j=PACK),
-                in_=src.rearrange("p j (c i) -> p c j i", i=4),
+                out=dst.rearrange("p (c e j) -> p c j e", e=4, j=PACK),
+                in_=src.rearrange("p j (c e) -> p c j e", e=4),
             )
 
-        def round_cols(dst, src, vector_cols):
-            width = src.shape[2]
-            interleave(nc.vector.tensor_copy, dst[:, : PACK * vector_cols], src[:, :, :vector_cols])
-            interleave(nc.scalar.copy, dst[:, PACK * vector_cols : PACK * width], src[:, :, vector_cols:])
+        def interleave_shared(dst, src, vector_cols):
+            if vector_cols > 0:
+                interleave(nc.vector.tensor_copy, dst[:, : PACK * vector_cols], src[:, :, :vector_cols])
+            interleave(nc.scalar.copy, dst[:, PACK * vector_cols :], src[:, :, vector_cols:])
+
+        def quantize(codes, scales, src):
+            nc.vector.quantize_mx(out=codes.bitcast(FP8X4), scales=scales, in_=src)
+
+        def round_x(g):
+            interleave_shared(x_bf[g][:], x_raw[g][:], X_VECTOR_COLS[g])
+
+        def quantize_x(g):
+            quantize(x_q[g][:], x_s[g][:], x_bf[g][:])
 
         def round_down(g, raw, m0, m1):
             src = raw[:].rearrange("p j (m i) -> p m j i", i=PACK)
@@ -142,23 +146,14 @@ def tile_mix_three_fm_pl_gelu_kernel(
 
         def quantize_down(g):
             for u in range(2):
-                cols = slice(u * R // 2, (u + 1) * R // 2)
-                nc.vector.quantize_mx(out=d_q[g][:, cols].bitcast(FP8X4), scales=d_s[g][:, cols], in_=d_bf[g][u][:])
+                cols = slice(2 * u * P, 2 * (u + 1) * P)
+                quantize(d_q[g][:, cols], d_s[g][:, cols], d_bf[g][u][:])
 
-        def quantize(codes, scales, src, c0, c1):
-            nc.vector.quantize_mx(
-                out=codes[:, c0:c1].bitcast(FP8X4), scales=scales[:, c0:c1], in_=src[:, PACK * c0 : PACK * c1]
-            )
-
-        def deal_scales(a):
-            src = ws_raw[:, :, a * KP : (a + 1) * KP].rearrange("p s (m i) -> p i s m", i=PACK)
-            nc.vector.tensor_copy(out=ws[a][:].rearrange("p s (i m) -> p i s m", i=PACK), in_=src)
-
-        def deal_up_scales():
-            nc.vector.tensor_copy(
-                out=us[:].rearrange("p (a i m) -> p i a m", a=HALVES, i=PACK),
-                in_=us_raw[:].rearrange("p (a m i) -> p i a m", a=HALVES, i=PACK),
-            )
+        def quantize_down_places(g, m0, m1):
+            for i in range(PACK):
+                cols = slice(i * P + m0, i * P + m1)
+                src = d_bf[g][i // 2][:, PACK * (i % 2 * P + m0) : PACK * (i % 2 * P + m1)]
+                quantize(d_q[g][:, cols], d_s[g][:, cols], src)
 
         def deal_w8(a):
             nc.vector.tensor_copy(
@@ -166,23 +161,33 @@ def tile_mix_three_fm_pl_gelu_kernel(
                 in_=w8_raw[a][:].bitcast(I32).rearrange("p g (m i) -> p g m i", i=PACK),
             )
 
-        def deal_w4(a):
+        def deal_fp4(a, u):
+            src = w4_raw[a][:].rearrange("p g (m i e) -> p g i m e", i=PACK, e=2)
             nc.vector.tensor_copy(
-                out=w4[a][:].rearrange("p g (i m e) -> p g i m e", i=PACK, e=2),
-                in_=w4_raw[a][:].rearrange("p g (m i e) -> p g i m e", i=PACK, e=2),
+                out=w4[a][u][:].rearrange("p g (i m e) -> p g i m e", i=2, e=2), in_=src[:, :, 2 * u : 2 * u + 2]
+            )
+            src = up_raw[a][:].rearrange("p (m i e) -> p i m e", i=PACK, e=2)
+            nc.vector.tensor_copy(
+                out=up[a][u][:].rearrange("p (i m e) -> p i m e", i=2, e=2), in_=src[:, 2 * u : 2 * u + 2]
             )
 
-        def deal_up(a):
+        def deal_scales(a):
             nc.vector.tensor_copy(
-                out=up[a][:].rearrange("p (i m e) -> p i m e", i=PACK, e=2),
-                in_=up_raw[a][:].rearrange("p (m i e) -> p i m e", i=PACK, e=2),
+                out=ws[a][:].rearrange("p g (i m) -> p i g m", i=PACK),
+                in_=ws_raw[:, :, a * KP : (a + 1) * KP].rearrange("p g (m i) -> p i g m", i=PACK),
+            )
+
+        def deal_up_scales():
+            nc.vector.tensor_copy(
+                out=us[:].rearrange("p (a i m) -> p i a m", a=HALVES, i=PACK),
+                in_=us_raw[:].rearrange("p (a m i) -> p i a m", a=HALVES, i=PACK),
             )
 
         h_acc = [ps.tile([P, PACK, TQ], F32, name="h_acc%d" % q, tag="bank%d" % q) for q in range(4)]
 
-        def h_pass(g, tiles):
-            for q in range(4):
-                for i in tiles:
+        def h_pass(g, banks=range(4), hands=range(PACK)):
+            for q in banks:
+                for i in hands:
                     nc.tensor.matmul_mx(
                         out=h_acc[q][:, i, :],
                         lhsT=d_q[g][:, i * P : (i + 1) * P].bitcast(FP8X4),
@@ -190,132 +195,131 @@ def tile_mix_three_fm_pl_gelu_kernel(
                         rhs=x_q[g][:, q * TQ : (q + 1) * TQ].bitcast(FP8X4),
                         rhs_scale=x_s[g][:, q * TQ : (q + 1) * TQ],
                         start=(g == 0 and i == 0),
-                        stop=(g == last and i == PACK - 1),
+                        stop=(g == LAST and i == TOP),
                     )
 
-        def y_pass(acc, a, i, g, c0=0, c1=T):
-            cols = slice(i * P, (i + 1) * P)
-            cols2 = slice(2 * i * P, 2 * (i + 1) * P)
-            if g < 2:
-                lhsT, lhsT_scale = w8[a][:, g, cols].bitcast(FP8X4), ws[a][4:P, g, cols]
-            elif g < PASSES:
-                lhsT, lhsT_scale = w4[a][:, g - 2, cols2].bitcast(FP4X4), ws[a][:, g - 2, cols]
-            else:
-                lhsT, lhsT_scale = up[a][:, cols2].bitcast(FP4X4), us[:, a * KP + i * P : a * KP + (i + 1) * P]
-            rhs, rhs_scale = (x_q[g], x_s[g]) if g < PASSES else (h_q, h_s)
-            step = TQ if g >= 2 and c1 - c0 < T else c1 - c0
-            for c in range(c0, c1, step):
-                nc.tensor.matmul_mx(
-                    out=acc[:, c - c0 : c - c0 + step],
-                    lhsT=lhsT,
-                    lhsT_scale=lhsT_scale,
-                    rhs=rhs[:, c : c + step].bitcast(FP8X4),
-                    rhs_scale=rhs_scale[:, c : c + step],
-                    start=(g == 0),
-                    stop=(g == PASSES and c + step == c1),
-                )
-
-        def h_out(q):
-            copy = nc.scalar.copy if q % 2 == 0 else nc.vector.tensor_copy
+        def h_out(copy, q):
             copy(
                 out=h_bf[:, q * TQ * PACK : (q + 1) * TQ * PACK].rearrange("p (t i) -> p t i", i=PACK),
                 in_=h_acc[q][:].rearrange("p i t -> p t i"),
             )
 
-        out_rows = out_0.rearrange("(a p i) t -> a p i t", p=P, i=PACK)
+        def y_passes(acc, a, i, passes, t0=0, t1=T):
+            places = slice(i * P, (i + 1) * P)
+            fp4_bytes = slice(i % 2 * 2 * P, (i % 2 + 1) * 2 * P)
+            for g in passes:
+                if g < W8_PASSES:
+                    lhsT, lhsT_scale = w8[a][:, g, places].bitcast(FP8X4), ws[a][W8_ROW:P, g, places]
+                elif g < UP_PASS:
+                    lhsT = w4[a][i // 2][:, g - W8_PASSES, fp4_bytes].bitcast(FP4X4)
+                    lhsT_scale = ws[a][:, g - W8_PASSES, places]
+                else:
+                    lhsT = up[a][i // 2][:, fp4_bytes].bitcast(FP4X4)
+                    lhsT_scale = us[:, a * KP + i * P : a * KP + (i + 1) * P]
+                rhs, rhs_scale = (x_q[g], x_s[g]) if g < UP_PASS else (h_q, h_s)
+                width = TQ if g >= W8_PASSES and t1 - t0 < T else t1 - t0
+                for t in range(t0, t1, width):
+                    nc.tensor.matmul_mx(
+                        out=acc[:, t - t0 : t - t0 + width],
+                        lhsT=lhsT,
+                        lhsT_scale=lhsT_scale,
+                        rhs=rhs[:, t : t + width].bitcast(FP8X4),
+                        rhs_scale=rhs_scale[:, t : t + width],
+                        start=(g == 0),
+                        stop=(g == UP_PASS and t + width == t1),
+                    )
 
-        def gelu(acc, a, i, c0, c1):
-            nc.scalar.activation(out=y[a][:, i, c0:c1], in_=acc[:], func=GELU, bias=bias[:, a, i : i + 1])
+        def gelu(acc, a, i, t0=0, t1=T):
+            nc.scalar.activation(out=y[a][:, i, t0:t1], in_=acc[:], func=GELU, bias=bias[:, a, i : i + 1])
 
-        def store_rows(a, i, c0=0, c1=T):
-            nc.sync.dma_start(out=out_rows[a, :, i, c0:c1], in_=y[a][:, i, c0:c1])
+        def store_rows(a, i):
+            rows = out_0.rearrange("(a p i) t -> a p i t", p=P, i=PACK)
+            nc.sync.dma_start(out=rows[a, :, i, :], in_=y[a][:, i, :])
 
-        def store_words(a, c0, c1):
-            dst = out_1[a].rearrange("p t i -> p (t i)").bitcast(I32)
-            nc.sync.dma_start(out=dst[:, c0:c1], in_=y_q[a][:, c0:c1].bitcast(I32))
+        def store_words(a):
+            nc.sync.dma_start(out=out_1[a].rearrange("p t j -> p (t j)").bitcast(I32), in_=y_q[a][:].bitcast(I32))
 
         acc0 = [ps.tile([P, T], F32, name="acc0_%d" % i, tag="bank%d" % (4 + i)) for i in range(PACK)]
 
-        round_cols(x_bf[0], x_raw[0], X_VECTOR_COLS)
-        quantize(x_q[0], x_s[0], x_bf[0], 0, T)
-        round_down(0, d_raw[0], 0, P)
-        quantize_down(0)
-        h_pass(0, range(PACK))
-        deal_w8(0)
-        deal_w4(0)
-        deal_up(0)
-        round_cols(x_bf[1], x_raw[1], X_VECTOR_COLS)
-        deal_scales(0)
-        quantize(x_q[1], x_s[1], x_bf[1], 0, T)
-        for g in range(2):
+        def half0_pass(g):
             for i in range(PACK):
-                y_pass(acc0[i], 0, i, g)
+                y_passes(acc0[i], 0, i, [g])
+
+        deal_w8(0)
+        for u in range(2):
+            deal_fp4(0, u)
+        round_x(0)
+        round_down(0, d_raw[0], 0, P)
+        quantize_x(0)
+        quantize_down(0)
+        h_pass(0)
+        round_x(1)
+        deal_scales(0)
+        quantize_x(1)
+        half0_pass(0)
+        half0_pass(1)
         round_down(1, d_raw[1], 0, P)
-        deal_up_scales()
-        quantize_down(1)
-        h_pass(1, range(PACK))
-        round_cols(x_bf[2], x_raw[2], X_VECTOR_COLS)
         deal_scales(1)
-        quantize(x_q[2], x_s[2], x_bf[2], 0, T)
-        for i in range(PACK):
-            y_pass(acc0[i], 0, i, 2)
+        quantize_down(1)
+        h_pass(1)
+        round_x(2)
+        deal_up_scales()
+        quantize_x(2)
+        half0_pass(2)
         round_down(2, d_raw[2], 0, P)
         quantize_down(2)
-        h_pass(2, range(PACK))
-        round_cols(x_bf[last], x_raw[last], LAST_VECTOR_COLS)
-        quantize(x_q[last], x_s[last], x_bf[last], 0, T)
-        for i in range(PACK):
-            y_pass(acc0[i], 0, i, last)
-        for h in range(2):
-            round_down(last, dl_raw[h], h * P // 2, (h + 1) * P // 2)
-        quantize_down(last)
-        for u in range(2):
-            h_pass(last, (2 * u, 2 * u + 1))
+        h_pass(2)
+        round_x(LAST)
+        quantize_x(LAST)
+        half0_pass(LAST)
+        for half in range(2):
+            round_down(LAST, d_last_raw[half], half * MH, (half + 1) * MH)
+            quantize_down_places(LAST, half * MH, (half + 1) * MH)
+        h_pass(LAST, (0, 1), (0, 1))
+        h_pass(LAST, (0, 1), (2, 3))
+        h_pass(LAST, (2, 3))
+
         deal_w8(1)
         for q in range(4):
-            h_out(q)
-        quantize(h_q, h_s, h_bf, 0, T)
-        deal_w4(1)
-        deal_up(1)
+            h_out(nc.vector.tensor_copy if q == 2 else nc.scalar.copy, q)
+        for t0 in (0, TH):
+            quantize(h_q[:, t0 : t0 + TH], h_s[:, t0 : t0 + TH], h_bf[:, PACK * t0 : PACK * (t0 + TH)])
+        for u in range(2):
+            deal_fp4(1, u)
 
-        top = PACK - 1
-        acc1 = [ps.tile([P, T], F32, name="acc1_%d" % i, tag="bank%d" % i) for i in range(top)]
-        acc_left = ps.tile([P, TH], F32, name="acc_left", tag="bank%d" % top)
-        for i in range(top):
-            for g in range(2):
-                y_pass(acc1[i], 1, i, g)
+        acc1 = [ps.tile([P, T], F32, name="acc1_%d" % i, tag="bank%d" % i) for i in range(TOP)]
+        acc_left = ps.tile([P, TH], F32, name="acc_left", tag="bank%d" % TOP)
+        w8_passes = range(W8_PASSES)
+        fp4_passes = range(W8_PASSES, UP_PASS + 1)
+        for i in range(TOP):
+            y_passes(acc1[i], 1, i, w8_passes)
         for i in range(PACK):
-            y_pass(acc0[i], 0, i, PASSES)
-            gelu(acc0[i], 0, i, 0, T)
+            y_passes(acc0[i], 0, i, [UP_PASS])
+            gelu(acc0[i], 0, i)
             store_rows(0, i)
-        for g in range(2):
-            y_pass(acc_left, 1, top, g, 0, TH)
+        y_passes(acc_left, 1, TOP, w8_passes, 0, TH)
         interleave(nc.vector.tensor_copy, y_bf[0][:], y[0][:])
-        quantize(y_q[0], y_s[:, 0, :], y_bf[0], 0, T)
-        for i in range(top):
-            for g in range(2, PASSES + 1):
-                y_pass(acc1[i], 1, i, g)
-            gelu(acc1[i], 1, i, 0, T)
+        quantize(y_q[0][:], y_s[:, 0, :], y_bf[0][:])
+        for i in range(TOP):
+            y_passes(acc1[i], 1, i, fp4_passes)
+            gelu(acc1[i], 1, i)
+            if i == TOP - 1:
+                store_words(0)
             store_rows(1, i)
-            if i == 1:
-                store_words(0, 0, T)
-        for g in range(2, PASSES + 1):
-            y_pass(acc_left, 1, top, g, 0, TH)
-        gelu(acc_left, 1, top, 0, TH)
-        store_rows(1, top, 0, TH)
+        y_passes(acc_left, 1, TOP, fp4_passes, 0, TH)
+        gelu(acc_left, 1, TOP, 0, TH)
         acc_right = ps.tile([P, TH], F32, name="acc_right", tag="bank4")
-        for g in range(PASSES + 1):
-            y_pass(acc_right, 1, top, g, TH, T)
+        y_passes(acc_right, 1, TOP, range(UP_PASS + 1), TH, T)
         interleave(nc.vector.tensor_copy, y_bf[1][:, : TH * PACK], y[1][:, :, :TH])
-        gelu(acc_right, 1, top, TH, T)
-        store_rows(1, top, TH, T)
-        round_cols(y_bf[1][:, TH * PACK :], y[1][:, :, TH:], OUT_VECTOR_COLS)
-        for h in range(2):
-            quantize(y_q[1], y_s[:, 1, :], y_bf[1], h * TH, (h + 1) * TH)
-            store_words(1, h * TH, (h + 1) * TH)
-        for q in range(QUADS):
-            eng = nc.sync if q % 2 == 0 else nc.scalar
-            eng.dma_start(
+        gelu(acc_right, 1, TOP, TH, T)
+        store_rows(1, TOP)
+        interleave_shared(y_bf[1][:, TH * PACK :], y[1][:, :, TH:], OUT_VECTOR_COLS)
+        for t0 in (0, TH):
+            quantize(y_q[1][:, t0 : t0 + TH], y_s[:, 1, t0 : t0 + TH], y_bf[1][:, PACK * t0 : PACK * (t0 + TH)])
+        store_words(1)
+        for q in range(P // QUAD):
+            engine = nc.sync if q % 2 == 0 else nc.scalar
+            engine.dma_start(
                 out=out_2.bitcast(I32)[:, 4 * q : 4 * q + 4, :].rearrange("a r t -> r a t"),
-                in_=y_s[32 * q : 32 * q + 4, :, :].bitcast(I32),
+                in_=y_s[QUAD * q : QUAD * q + 4, :, :].bitcast(I32),
             )

@@ -29,7 +29,7 @@ TQ = T // 4
 TH = T // 2
 MH = P // 2
 
-X_VECTOR_COLS = (0, 0, 128, 320)
+X_VECTOR_COLS = (0, 0, 192, 320)
 OUT_VECTOR_COLS = 160
 
 
@@ -88,6 +88,8 @@ def tile_mix_three_fm_pl_gelu_kernel(
             load(w8_raw[a][:].bitcast(I32), src.bitcast(I32))
             src = w4_words[:, :, 2 * a * KP : 2 * (a + 1) * KP].rearrange("g p c -> p g c")
             load(w4_raw[a][:].bitcast(I32), src.bitcast(I32))
+
+        def load_up(a):
             load(up_raw[a][:].bitcast(I32), up_words[0, :, 2 * a * KP : 2 * (a + 1) * KP].bitcast(I32))
 
         def load_scales(engine, dst, first_row, scales):
@@ -105,10 +107,11 @@ def tile_mix_three_fm_pl_gelu_kernel(
         load_scales(nc.gpsimd, ws_words, W8_ROW, w8_scales)
         load_weights(0)
         load(x_raw[0][:], pass_rows(x, 0))
-        load_scales(nc.scalar, ws_words, 0, w4_scales)
         load(d_raw[0][:], pass_rows(down, 0))
+        load_scales(nc.scalar, ws_words, 0, w4_scales)
         load(x_raw[1][:], pass_rows(x, 1))
         load(d_raw[1][:], pass_rows(down, 1))
+        load_up(0)
         load_scales(nc.sync, us_words, 0, up_scales)
         load(x_raw[2][:], pass_rows(x, 2))
         load(d_raw[2][:], pass_rows(down, 2))
@@ -116,6 +119,7 @@ def tile_mix_three_fm_pl_gelu_kernel(
         for half in range(2):
             load(d_last_raw[half][:], pass_rows(down, LAST)[:, :, half * R // 2 : (half + 1) * R // 2])
         load_weights(1)
+        load_up(1)
         load(bias[:], b.rearrange("(a p i) -> p a i", p=P, i=PACK))
 
         def interleave(copy, dst, src):
@@ -161,11 +165,13 @@ def tile_mix_three_fm_pl_gelu_kernel(
                 in_=w8_raw[a][:].bitcast(I32).rearrange("p g (m i) -> p g m i", i=PACK),
             )
 
-        def deal_fp4(a, u):
+        def deal_w4(a, u):
             src = w4_raw[a][:].rearrange("p g (m i e) -> p g i m e", i=PACK, e=2)
             nc.vector.tensor_copy(
                 out=w4[a][u][:].rearrange("p g (i m e) -> p g i m e", i=2, e=2), in_=src[:, :, 2 * u : 2 * u + 2]
             )
+
+        def deal_up(a, u):
             src = up_raw[a][:].rearrange("p (m i e) -> p i m e", i=PACK, e=2)
             nc.vector.tensor_copy(
                 out=up[a][u][:].rearrange("p (i m e) -> p i m e", i=2, e=2), in_=src[:, 2 * u : 2 * u + 2]
@@ -232,9 +238,9 @@ def tile_mix_three_fm_pl_gelu_kernel(
         def gelu(acc, a, i, t0=0, t1=T):
             nc.scalar.activation(out=y[a][:, i, t0:t1], in_=acc[:], func=GELU, bias=bias[:, a, i : i + 1])
 
-        def store_rows(a, i):
+        def store_rows(a, i0, i1):
             rows = out_0.rearrange("(a p i) t -> a p i t", p=P, i=PACK)
-            nc.sync.dma_start(out=rows[a, :, i, :], in_=y[a][:, i, :])
+            nc.sync.dma_start(out=rows[a, :, i0:i1, :], in_=y[a][:, i0:i1, :])
 
         def store_words(a):
             nc.sync.dma_start(out=out_1[a].rearrange("p t j -> p (t j)").bitcast(I32), in_=y_q[a][:].bitcast(I32))
@@ -247,21 +253,23 @@ def tile_mix_three_fm_pl_gelu_kernel(
 
         deal_w8(0)
         for u in range(2):
-            deal_fp4(0, u)
+            deal_w4(0, u)
         round_x(0)
         round_down(0, d_raw[0], 0, P)
         quantize_x(0)
         quantize_down(0)
         h_pass(0)
         round_x(1)
-        deal_scales(0)
+        for a in range(HALVES):
+            deal_scales(a)
         quantize_x(1)
         half0_pass(0)
-        half0_pass(1)
         round_down(1, d_raw[1], 0, P)
-        deal_scales(1)
+        deal_up(0, 0)
         quantize_down(1)
         h_pass(1)
+        half0_pass(1)
+        deal_up(0, 1)
         round_x(2)
         deal_up_scales()
         quantize_x(2)
@@ -285,7 +293,8 @@ def tile_mix_three_fm_pl_gelu_kernel(
         for t0 in (0, TH):
             quantize(h_q[:, t0 : t0 + TH], h_s[:, t0 : t0 + TH], h_bf[:, PACK * t0 : PACK * (t0 + TH)])
         for u in range(2):
-            deal_fp4(1, u)
+            deal_w4(1, u)
+            deal_up(1, u)
 
         acc1 = [ps.tile([P, T], F32, name="acc1_%d" % i, tag="bank%d" % i) for i in range(TOP)]
         acc_left = ps.tile([P, TH], F32, name="acc_left", tag="bank%d" % TOP)
@@ -296,23 +305,23 @@ def tile_mix_three_fm_pl_gelu_kernel(
         for i in range(PACK):
             y_passes(acc0[i], 0, i, [UP_PASS])
             gelu(acc0[i], 0, i)
-            store_rows(0, i)
+            store_rows(0, i, i + 1)
         y_passes(acc_left, 1, TOP, w8_passes, 0, TH)
         interleave(nc.vector.tensor_copy, y_bf[0][:], y[0][:])
         quantize(y_q[0][:], y_s[:, 0, :], y_bf[0][:])
         for i in range(TOP):
             y_passes(acc1[i], 1, i, fp4_passes)
             gelu(acc1[i], 1, i)
-            if i == TOP - 1:
-                store_words(0)
-            store_rows(1, i)
+        store_rows(1, 0, 2)
+        store_words(0)
+        store_rows(1, 2, TOP)
         y_passes(acc_left, 1, TOP, fp4_passes, 0, TH)
         gelu(acc_left, 1, TOP, 0, TH)
         acc_right = ps.tile([P, TH], F32, name="acc_right", tag="bank4")
         y_passes(acc_right, 1, TOP, range(UP_PASS + 1), TH, T)
         interleave(nc.vector.tensor_copy, y_bf[1][:, : TH * PACK], y[1][:, :, :TH])
         gelu(acc_right, 1, TOP, TH, T)
-        store_rows(1, TOP)
+        store_rows(1, TOP, PACK)
         interleave_shared(y_bf[1][:, TH * PACK :], y[1][:, :, TH:], OUT_VECTOR_COLS)
         for t0 in (0, TH):
             quantize(y_q[1][:, t0 : t0 + TH], y_s[:, 1, t0 : t0 + TH], y_bf[1][:, PACK * t0 : PACK * (t0 + TH)])

from contextlib import ExitStack

import concourse.mybir as mybir

K, R, M, T = 2048, 512, 1024, 512
FLOPS = 2 * T * (K * R + K * M + R * M)

F32 = mybir.dt.float32
BF16 = mybir.dt.bfloat16
I32 = mybir.dt.int32
U32 = mybir.dt.uint32
U8 = mybir.dt.uint8
FP8X4 = mybir.dt.float8_e4m3fn_x4
FP4X4 = mybir.dt.float4_e2m1fn_x4
GELU = mybir.ActivationFunctionType.Gelu_apprx_tanh

P = 128
PACK = 4
KP = P * PACK
PASSES = K // KP
W8_PASSES = 2
UP_PASS = PASSES
LAST = PASSES - 1
TOP = PACK - 1
HALVES = M // KP
QUAD = 32
W8_ROW = 4
TQ = T // 4
TH = T // 2
MH = P // 2

X_VECTOR_COLS = (0, 0, 192, 320)
OUT_VECTOR_COLS = 160


def tile_mix_three_fm_pl_gelu_kernel(
    tc, x, w8_words, w8_scales, w4_words, w4_scales, down, up_words, up_scales, b, out_0, out_1, out_2
):
    nc = tc.nc
    with ExitStack() as ctx:
        sb = ctx.enter_context(tc.tile_pool(name="sb", bufs=1))
        ps = ctx.enter_context(tc.psum_pool(name="ps", bufs=1))
        ctx.enter_context(tc.manual_schedule())

        def tile(name, shape, dtype):
            return sb.tile(shape, dtype, name=name, align_bytes=64)

        def tiles(name, count, shape, dtype):
            return [tile("%s%d" % (name, n), shape, dtype) for n in range(count)]

        x_raw = tiles("x_raw", PASSES, [P, PACK, T], F32)
        x_bf = tiles("x_bf", PASSES, [P, T * PACK], BF16)
        x_q = tiles("x_q", PASSES, [P, T], U32)
        x_s = tiles("x_s", PASSES, [P, T], U8)
        d_raw = tiles("d_raw", LAST, [P, PACK, R], F32)
        d_last_raw = tiles("d_last_raw", 2, [P, PACK, R // 2], F32)
        d_bf = [tiles("d_bf%d_" % g, 2, [P, 2 * KP], BF16) for g in range(PASSES)]
        d_q = tiles("d_q", PASSES, [P, R], U32)
        d_s = tiles("d_s", PASSES, [P, R], U8)
        w8_raw = tiles("w8_raw", HALVES, [P, 2, KP], U32)
        w8 = tiles("w8_", HALVES, [P, 2, KP], U32)
        w4_raw = tiles("w4_raw", HALVES, [P, 2, 2 * KP], U8)
        w4 = [tiles("w4_%d_" % a, 2, [P, 2, KP], U8) for a in range(HALVES)]
        up_raw = tiles("up_raw", HALVES, [P, 2 * KP], U8)
        up = [tiles("up_%d_" % a, 2, [P, KP], U8) for a in range(HALVES)]
        ws_raw = tile("ws_raw", [P, 2, M], U8)
        ws = tiles("ws_", HALVES, [P, 2, KP], U8)
        us_raw = tile("us_raw", [P, M], U8)
        us = tile("us", [P, M], U8)
        bias = tile("bias", [P, HALVES, PACK], F32)
        warm = tile("warm", [P, 8], F32)
        h_bf = tile("h_bf", [P, T * PACK], BF16)
        h_q = tile("h_q", [P, T], U32)
        h_s = tile("h_s", [P, T], U8)
        y = tiles("y", HALVES, [P, PACK, T], F32)
        y_bf = tiles("y_bf", HALVES, [P, T * PACK], BF16)
        y_q = tiles("y_q", HALVES, [P, T], U32)
        y_s = tile("y_s", [P, HALVES, T], U8)

        def pass_rows(src, g):
            return src[g * KP : (g + 1) * KP, :].rearrange("(p j) c -> p j c", j=PACK)

        def load(dst, src):
            nc.sync.dma_start(out=dst, in_=src)

        def load_weights(a):
            src = w8_words[:, :, a * KP : (a + 1) * KP, :].rearrange("g p n j -> p g (n j)")
            load(w8_raw[a][:].bitcast(I32), src.bitcast(I32))
            src = w4_words[:, :, 2 * a * KP : 2 * (a + 1) * KP].rearrange("g p c -> p g c")
            load(w4_raw[a][:].bitcast(I32), src.bitcast(I32))

        def load_up(a):
            load(up_raw[a][:].bitcast(I32), up_words[0, :, 2 * a * KP : 2 * (a + 1) * KP].bitcast(I32))

        def load_scales(engine, dst, first_row, scales):
            src = scales.bitcast(I32).rearrange("g (q r) n -> r q g n", r=4)
            for r in range(4):
                engine.dma_start(out=dst[first_row + r : P : QUAD], in_=src[r])

        ws_words = ws_raw[:].bitcast(I32)
        us_words = us_raw[:].bitcast(I32).rearrange("p (g n) -> p g n", g=1)
        nc.vector.memset(ws_words, 0)
        nc.vector.memset(us_words, 0)
        nc.vector.memset(warm[:], 0.0)
        nc.scalar.activation(out=warm[:], in_=warm[:], func=GELU)

        load_scales(nc.gpsimd, ws_words, W8_ROW, w8_scales)
        load_weights(0)
        load(x_raw[0][:], pass_rows(x, 0))
        load(d_raw[0][:], pass_rows(down, 0))
        load_scales(nc.scalar, ws_words, 0, w4_scales)
        load(x_raw[1][:], pass_rows(x, 1))
        load(d_raw[1][:], pass_rows(down, 1))
        load_up(0)
        load_scales(nc.sync, us_words, 0, up_scales)
        load(x_raw[2][:], pass_rows(x, 2))
        load(d_raw[2][:], pass_rows(down, 2))
        load(x_raw[LAST][:], pass_rows(x, LAST))
        for half in range(2):
            load(d_last_raw[half][:], pass_rows(down, LAST)[:, :, half * R // 2 : (half + 1) * R // 2])
        load_weights(1)
        load_up(1)
        load(bias[:], b.rearrange("(a p i) -> p a i", p=P, i=PACK))

        def interleave(copy, dst, src):
            copy(
                out=dst.rearrange("p (c e j) -> p c j e", e=4, j=PACK),
                in_=src.rearrange("p j (c e) -> p c j e", e=4),
            )

        def interleave_shared(dst, src, vector_cols):
            if vector_cols > 0:
                interleave(nc.vector.tensor_copy, dst[:, : PACK * vector_cols], src[:, :, :vector_cols])
            interleave(nc.scalar.copy, dst[:, PACK * vector_cols :], src[:, :, vector_cols:])

        def quantize(codes, scales, src):
            nc.vector.quantize_mx(out=codes.bitcast(FP8X4), scales=scales, in_=src)

        def round_x(g):
            interleave_shared(x_bf[g][:], x_raw[g][:], X_VECTOR_COLS[g])

        def quantize_x(g):
            quantize(x_q[g][:], x_s[g][:], x_bf[g][:])

        def round_down(g, raw, m0, m1):
            src = raw[:].rearrange("p j (m i) -> p m j i", i=PACK)
            for u, copy in enumerate((nc.vector.tensor_copy, nc.scalar.copy)):
                dst = d_bf[g][u][:].rearrange("p (i m j) -> p m j i", i=2, j=PACK)
                copy(out=dst[:, m0:m1, :, :], in_=src[:, :, :, 2 * u : 2 * u + 2])

        def quantize_down(g):
            for u in range(2):
                cols = slice(2 * u * P, 2 * (u + 1) * P)
                quantize(d_q[g][:, cols], d_s[g][:, cols], d_bf[g][u][:])

        def quantize_down_places(g, m0, m1):
            for i in range(PACK):
                cols = slice(i * P + m0, i * P + m1)
                src = d_bf[g][i // 2][:, PACK * (i % 2 * P + m0) : PACK * (i % 2 * P + m1)]
                quantize(d_q[g][:, cols], d_s[g][:, cols], src)

        def deal_w8(a):
            nc.vector.tensor_copy(
                out=w8[a][:].bitcast(I32).rearrange("p g (i m) -> p g m i", i=PACK),
                in_=w8_raw[a][:].bitcast(I32).rearrange("p g (m i) -> p g m i", i=PACK),
            )

        def deal_w4(a, u):
            src = w4_raw[a][:].rearrange("p g (m i e) -> p g i m e", i=PACK, e=2)
            nc.vector.tensor_copy(
                out=w4[a][u][:].rearrange("p g (i m e) -> p g i m e", i=2, e=2), in_=src[:, :, 2 * u : 2 * u + 2]
            )

        def deal_up(a, u):
            src = up_raw[a][:].rearrange("p (m i e) -> p i m e", i=PACK, e=2)
            nc.vector.tensor_copy(
                out=up[a][u][:].rearrange("p (i m e) -> p i m e", i=2, e=2), in_=src[:, 2 * u : 2 * u + 2]
            )

        def deal_scales(a):
            nc.vector.tensor_copy(
                out=ws[a][:].rearrange("p g (i m) -> p i g m", i=PACK),
                in_=ws_raw[:, :, a * KP : (a + 1) * KP].rearrange("p g (m i) -> p i g m", i=PACK),
            )

        def deal_up_scales():
            nc.vector.tensor_copy(
                out=us[:].rearrange("p (a i m) -> p i a m", a=HALVES, i=PACK),
                in_=us_raw[:].rearrange("p (a m i) -> p i a m", a=HALVES, i=PACK),
            )

        h_acc = [ps.tile([P, PACK, TQ], F32, name="h_acc%d" % q, tag="bank%d" % q) for q in range(4)]

        def h_pass(g, banks=range(4), hands=range(PACK)):
            for q in banks:
                for i in hands:
                    nc.tensor.matmul_mx(
                        out=h_acc[q][:, i, :],
                        lhsT=d_q[g][:, i * P : (i + 1) * P].bitcast(FP8X4),
                        lhsT_scale=d_s[g][:, i * P : (i + 1) * P],
                        rhs=x_q[g][:, q * TQ : (q + 1) * TQ].bitcast(FP8X4),
                        rhs_scale=x_s[g][:, q * TQ : (q + 1) * TQ],
                        start=(g == 0 and i == 0),
                        stop=(g == LAST and i == TOP),
                    )

        def h_out(copy, q):
            copy(
                out=h_bf[:, q * TQ * PACK : (q + 1) * TQ * PACK].rearrange("p (t i) -> p t i", i=PACK),
                in_=h_acc[q][:].rearrange("p i t -> p t i"),
            )

        def y_passes(acc, a, i, passes, t0=0, t1=T):
            places = slice(i * P, (i + 1) * P)
            fp4_bytes = slice(i % 2 * 2 * P, (i % 2 + 1) * 2 * P)
            for g in passes:
                if g < W8_PASSES:
                    lhsT, lhsT_scale = w8[a][:, g, places].bitcast(FP8X4), ws[a][W8_ROW:P, g, places]
                elif g < UP_PASS:
                    lhsT = w4[a][i // 2][:, g - W8_PASSES, fp4_bytes].bitcast(FP4X4)
                    lhsT_scale = ws[a][:, g - W8_PASSES, places]
                else:
                    lhsT = up[a][i // 2][:, fp4_bytes].bitcast(FP4X4)
                    lhsT_scale = us[:, a * KP + i * P : a * KP + (i + 1) * P]
                rhs, rhs_scale = (x_q[g], x_s[g]) if g < UP_PASS else (h_q, h_s)
                width = TQ if g >= W8_PASSES and t1 - t0 < T else t1 - t0
                for t in range(t0, t1, width):
                    nc.tensor.matmul_mx(
                        out=acc[:, t - t0 : t - t0 + width],
                        lhsT=lhsT,
                        lhsT_scale=lhsT_scale,
                        rhs=rhs[:, t : t + width].bitcast(FP8X4),
                        rhs_scale=rhs_scale[:, t : t + width],
                        start=(g == 0),
                        stop=(g == UP_PASS and t + width == t1),
                    )

        def gelu(acc, a, i, t0=0, t1=T):
            nc.scalar.activation(out=y[a][:, i, t0:t1], in_=acc[:], func=GELU, bias=bias[:, a, i : i + 1])

        def store_rows(a, i0, i1):
            rows = out_0.rearrange("(a p i) t -> a p i t", p=P, i=PACK)
            nc.sync.dma_start(out=rows[a, :, i0:i1, :], in_=y[a][:, i0:i1, :])

        def store_words(a):
            nc.sync.dma_start(out=out_1[a].rearrange("p t j -> p (t j)").bitcast(I32), in_=y_q[a][:].bitcast(I32))

        acc0 = [ps.tile([P, T], F32, name="acc0_%d" % i, tag="bank%d" % (4 + i)) for i in range(PACK)]

        def half0_pass(g):
            for i in range(PACK):
                y_passes(acc0[i], 0, i, [g])

        deal_w8(0)
        for u in range(2):
            deal_w4(0, u)
        round_x(0)
        round_down(0, d_raw[0], 0, P)
        quantize_x(0)
        quantize_down(0)
        h_pass(0)
        round_x(1)
        for a in range(HALVES):
            deal_scales(a)
        quantize_x(1)
        half0_pass(0)
        round_down(1, d_raw[1], 0, P)
        deal_up(0, 0)
        quantize_down(1)
        h_pass(1)
        half0_pass(1)
        deal_up(0, 1)
        round_x(2)
        deal_up_scales()
        quantize_x(2)
        half0_pass(2)
        round_down(2, d_raw[2], 0, P)
        quantize_down(2)
        h_pass(2)
        round_x(LAST)
        quantize_x(LAST)
        half0_pass(LAST)
        for half in range(2):
            round_down(LAST, d_last_raw[half], half * MH, (half + 1) * MH)
            quantize_down_places(LAST, half * MH, (half + 1) * MH)
        h_pass(LAST, (0, 1), (0, 1))
        h_pass(LAST, (0, 1), (2, 3))
        h_pass(LAST, (2, 3))

        deal_w8(1)
        for q in range(4):
            h_out(nc.vector.tensor_copy if q == 2 else nc.scalar.copy, q)
        for t0 in (0, TH):
            quantize(h_q[:, t0 : t0 + TH], h_s[:, t0 : t0 + TH], h_bf[:, PACK * t0 : PACK * (t0 + TH)])
        for u in range(2):
            deal_w4(1, u)
            deal_up(1, u)

        acc1 = [ps.tile([P, T], F32, name="acc1_%d" % i, tag="bank%d" % i) for i in range(TOP)]
        acc_left = ps.tile([P, TH], F32, name="acc_left", tag="bank%d" % TOP)
        w8_passes = range(W8_PASSES)
        fp4_passes = range(W8_PASSES, UP_PASS + 1)
        for i in range(TOP):
            y_passes(acc1[i], 1, i, w8_passes)
        for i in range(PACK):
            y_passes(acc0[i], 0, i, [UP_PASS])
            gelu(acc0[i], 0, i)
            store_rows(0, i, i + 1)
        y_passes(acc_left, 1, TOP, w8_passes, 0, TH)
        interleave(nc.vector.tensor_copy, y_bf[0][:], y[0][:])
        quantize(y_q[0][:], y_s[:, 0, :], y_bf[0][:])
        for i in range(TOP):
            y_passes(acc1[i], 1, i, fp4_passes)
            gelu(acc1[i], 1, i)
        store_rows(1, 0, 2)
        store_words(0)
        store_rows(1, 2, TOP)
        y_passes(acc_left, 1, TOP, fp4_passes, 0, TH)
        gelu(acc_left, 1, TOP, 0, TH)
        acc_right = ps.tile([P, TH], F32, name="acc_right", tag="bank4")
        y_passes(acc_right, 1, TOP, range(UP_PASS + 1), TH, T)
        interleave(nc.vector.tensor_copy, y_bf[1][:, : TH * PACK], y[1][:, :, :TH])
        gelu(acc_right, 1, TOP, TH, T)
        store_rows(1, TOP, PACK)
        interleave_shared(y_bf[1][:, TH * PACK :], y[1][:, :, TH:], OUT_VECTOR_COLS)
        for t0 in (0, TH):
            quantize(y_q[1][:, t0 : t0 + TH], y_s[:, 1, t0 : t0 + TH], y_bf[1][:, PACK * t0 : PACK * (t0 + TH)])
        store_words(1)
        for q in range(P // QUAD):
            engine = nc.sync if q % 2 == 0 else nc.scalar
            engine.dma_start(
                out=out_2.bitcast(I32)[:, 4 * q : 4 * q + 4, :].rearrange("a r t -> r a t"),
                in_=y_s[QUAD * q : QUAD * q + 4, :, :].bitcast(I32),
            )
